import numpy as np, ml_dtypes
CORES = [3,5,19,21,35,37,51,53,67,69]
N = 10
WB, KB, QP = 2, 1, 128
def setup_inputs(rng):
    return {"q": rng.standard_normal((N, 128, QP), dtype=np.float32).astype(ml_dtypes.bfloat16), "k": rng.standard_normal((N, 128, KB * 128), dtype=np.float32).astype(ml_dtypes.bfloat16), "v": rng.standard_normal((N, 128, KB * 128), dtype=np.float32).astype(ml_dtypes.bfloat16)}
def setup_inputs_big(rng):
    d = setup_inputs(rng)
    for k in ("q", "k", "v"): d[k] = (d[k].astype(np.float32) * 1024.0).astype(d[k].dtype)
    return d
def setup_inputs_small(rng):
    d = setup_inputs(rng)
    for k in ("q", "k", "v"): d[k] = (d[k].astype(np.float32) * (1 / 1024.0)).astype(d[k].dtype)
    return d
def setup_inputs_apart(rng):
    d = setup_inputs(rng)
    f = (10.0 ** rng.permutation(np.linspace(-1.5, 1.5, N))).astype(np.float32).reshape(N, 1, 1)
    for k in ("q", "k", "v"): d[k] = (d[k].astype(np.float32) * f).astype(d[k].dtype)
    return d
def reference(q, k, v):
    Q, K, V = q.astype(np.float64), k.astype(np.float64), v.astype(np.float64)
    y = np.zeros((N, 128, QP))
    for r in range(N):
        for j in range(max(0, r - WB), r + 1):
            for b in range(KB):
                S = np.maximum(K[j][:, 128 * b:128 * b + 128].T @ Q[r], 0.0)
                y[r] += V[j][:, 128 * b:128 * b + 128].T @ S
    return {"y": y.astype(ml_dtypes.bfloat16 if q.dtype != np.float64 else np.float64)}

@@ -1,0 +1,114 @@
+from concourse.bass import DstId, RemoteDMATransfer
+from concourse.mybir import AluOpType
+
+WB = 2
+D = 128
+SEND_ENGINES = 8
+
+SCRATCH = {
+    "kv": ("sbuf", [128, 2 * D], "bfloat16"),
+    "qs": ("sbuf", [128, D], "bfloat16"),
+    "land1": ("sbuf", [128, 2 * D], "bfloat16"),
+    "land2": ("sbuf", [128, 2 * D], "bfloat16"),
+    "zero": ("sbuf", [128, D], "float32"),
+    "s0": ("sbuf", [128, D], "bfloat16"),
+    "s1": ("sbuf", [128, D], "bfloat16"),
+    "s2": ("sbuf", [128, D], "bfloat16"),
+    "ys": ("sbuf", [128, D], "bfloat16"),
+    "ps0": ("psum", [128, 512], "float32"),
+    "ps1": ("psum", [128, 512], "float32"),
+    "ps2": ("psum", [128, 512], "float32"),
+    "po": ("psum", [128, 512], "float32"),
+}
+SEMAPHORES = ["kvl", "ql", "zf", "sent", "arr1", "arr2", "sm0", "sm1", "sm2", "rl0", "rl1", "rl2", "om", "cp", "stored"]
+
+
+def _engines(mask):
+    return [e for e in range(mask.bit_length()) if (mask >> e) & 1]
+
+
+def _plan(T, topo, r):
+    src = T.cores[r]
+    dsts = [(d, T.cores[r + d]) for d in range(1, WB + 1) if r + d < len(T.cores)]
+    if not dsts:
+        return {}
+    pool = topo.mask(src, dsts[0][1])
+    for _, c in dsts:
+        pool &= topo.mask(src, c)
+    eng = _engines(pool)[:SEND_ENGINES]
+    per = 1
+    while per * 2 * len(dsts) <= len(eng):
+        per *= 2
+    out = {}
+    for i, (d, c) in enumerate(dsts):
+        out[d] = (c, sum(1 << e for e in eng[i * per:(i + 1) * per]), per)
+    return out
+
+
+def _far(topo, src, dst):
+    if topo.chip(src) == topo.chip(dst):
+        return 0
+    return 1 if topo.die(src) == topo.die(dst) else 2
+
+
+def rank_program(g, core, T, topo):
+    r = T.rank_of(core)
+    if r is None:
+        return
+    sem = T.sem
+    te, ve = g.tensor, g.vector
+
+    g.sync.dma_start(T.kv[:, 0:D], T.k[:]).then_inc(sem.kvl, 16)
+    g.scalar.dma_start(T.kv[:, D:2 * D], T.v[:]).then_inc(sem.kvl, 16)
+    g.sync.dma_start(T.qs[:], T.q[:]).then_inc(sem.ql, 16)
+    ve.memset(T.zero[:], 0.0).then_inc(sem.zf, 1)
+
+    plan = _plan(T, topo, r)
+    if plan:
+        trs = []
+        total = 0
+        for d in sorted(plan):
+            dst, mask, cnt = plan[d]
+            assert topo.may_write(core, dst)
+            rid, pid, _ = topo.addr(dst)
+            trs.append(RemoteDMATransfer(dst_ids=[DstId(rid=rid, pnc=pid)], dma_engine_mask=mask,
+                                         remote_sem=sem["arr%d" % d], src=T.kv[:], dst=T["land%d" % d][:]))
+            total += cnt
+        g.wait_ge(sem.kvl, 32)
+        g.remote_dma_fused(trs, local_sem=sem.sent)
+
+    srcs = sorted([d for d in range(1, WB + 1) if r - d >= 0], key=lambda d: (_far(topo, T.cores[r - d], core), d))
+    blocks = [(T.kv, None, 0)] + [(T["land%d" % d], sem["arr%d" % d], _plan(T, topo, r - d)[d][2]) for d in srcs]
+    nb = len(blocks)
+
+    def s_product(i):
+        buf, arr, cnt = blocks[i]
+        if arr is not None:
+            te.wait_ge(arr, cnt)
+        te.matmul(T["ps%d" % i][:, 0:D], buf[:, 0:D], T.qs[:], True, True).then_inc(sem["sm%d" % i], 1)
+
+    def o_product(i):
+        te.wait_ge(sem["rl%d" % i], 1)
+        te.matmul(T.po[:, 0:D], blocks[i][0][:, D:2 * D], T["s%d" % i][:], i == 0, i == nb - 1).then_inc(sem.om, 1)
+
+    te.wait_ge(sem.kvl, 32)
+    te.wait_ge(sem.ql, 16)
+    s_product(0)
+    o_product(0)
+    for i in range(1, nb):
+        s_product(i)
+    for i in range(1, nb):
+        o_product(i)
+
+    ve.wait_ge(sem.zf, 1)
+    for i in range(nb):
+        ve.wait_ge(sem["sm%d" % i], 1)
+        ve.tensor_tensor(T["s%d" % i][:], T["ps%d" % i][:, 0:D], T.zero[:], AluOpType.max).then_inc(sem["rl%d" % i], 1)
+    ve.wait_ge(sem.om, nb)
+    ve.tensor_copy(T.ys[:], T.po[:, 0:D]).then_inc(sem.cp, 1)
+
+    g.sync.wait_ge(sem.cp, 1)
+    g.sync.dma_start(T.y[:], T.ys[:]).then_inc(sem.stored, 16)
+    g.sync.wait_ge(sem.stored, 16)
+    if plan:
+        g.wait_ge(sem.sent, total)

@@ -1,47 +1,52 @@
-from concourse.bass import DstId, RemoteDMATransfer
 from concourse.mybir import AluOpType
 
 WB = 2
 D = 128
-SEND_ENGINES = 8
+H = D // 2
+PER = 8
 
 SCRATCH = {
     "kv": ("sbuf", [128, 2 * D], "bfloat16"),
     "qs": ("sbuf", [128, D], "bfloat16"),
     "land1": ("sbuf", [128, 2 * D], "bfloat16"),
     "land2": ("sbuf", [128, 2 * D], "bfloat16"),
-    "zero": ("sbuf", [128, D], "float32"),
+    "zero": ("sbuf", [128, H], "float32"),
     "s0": ("sbuf", [128, D], "bfloat16"),
     "s1": ("sbuf", [128, D], "bfloat16"),
     "s2": ("sbuf", [128, D], "bfloat16"),
     "ys": ("sbuf", [128, D], "bfloat16"),
-    "ps0": ("psum", [128, 512], "float32"),
-    "ps1": ("psum", [128, 512], "float32"),
-    "ps2": ("psum", [128, 512], "float32"),
-    "po": ("psum", [128, 512], "float32"),
 }
-SEMAPHORES = ["kvl", "ql", "zf", "sent", "arr1", "arr2", "sm0", "sm1", "sm2", "rl0", "rl1", "rl2", "om", "cp", "stored"]
+SEMAPHORES = ["kvl", "ql", "zf", "sent", "ka1", "ka2", "va1", "va2", "cp", "stored"]
+for _h in range(2):
+    SCRATCH["po%d" % _h] = ("psum", [128, 512], "float32")
+    SEMAPHORES.append("om%d" % _h)
+    for _i in range(WB + 1):
+        SCRATCH["ps%d%d" % (_i, _h)] = ("psum", [128, 512], "float32")
+        SEMAPHORES += ["sm%d%d" % (_i, _h), "rl%d%d" % (_i, _h)]
 
 
 def _engines(mask):
     return [e for e in range(mask.bit_length()) if (mask >> e) & 1]
 
 
-def _plan(T, topo, r):
+def _pieces(T, topo, r):
     src = T.cores[r]
     dsts = [(d, T.cores[r + d]) for d in range(1, WB + 1) if r + d < len(T.cores)]
-    if not dsts:
-        return {}
-    pool = topo.mask(src, dsts[0][1])
-    for _, c in dsts:
-        pool &= topo.mask(src, c)
-    eng = _engines(pool)[:SEND_ENGINES]
-    per = 1
-    while per * 2 * len(dsts) <= len(eng):
-        per *= 2
-    out = {}
-    for i, (d, c) in enumerate(dsts):
-        out[d] = (c, sum(1 << e for e in eng[i * per:(i + 1) * per]), per)
+    dsts.sort(key=lambda x: (len(_engines(topo.mask(src, x[1]))), x[0]))
+    used, lane, line, out = [], [], 0, []
+    for d, c in dsts:
+        free = [e for e in _engines(topo.mask(src, c)) if e not in used]
+        if len(free) >= PER:
+            lane, line = free[:PER], 0
+            used += lane
+            cuts = [(0, 2 * D, "ka")]
+        else:
+            cuts = [(0, D, "ka"), (D, 2 * D, "va")]
+        mask = sum(1 << e for e in lane)
+        assert mask & topo.mask(src, c) == mask
+        for lo, hi, name in cuts:
+            line += hi - lo
+            out.append((d, c, lo, hi, mask, len(lane), "%s%d" % (name, d), line))
     return out
 
 
@@ -63,33 +68,43 @@ def rank_program(g, core, T, topo):
     g.sync.dma_start(T.qs[:], T.q[:]).then_inc(sem.ql, 16)
     ve.memset(T.zero[:], 0.0).then_inc(sem.zf, 1)
 
-    plan = _plan(T, topo, r)
-    if plan:
-        trs = []
-        total = 0
-        for d in sorted(plan):
-            dst, mask, cnt = plan[d]
-            assert topo.may_write(core, dst)
-            rid, pid, _ = topo.addr(dst)
-            trs.append(RemoteDMATransfer(dst_ids=[DstId(rid=rid, pnc=pid)], dma_engine_mask=mask,
-                                         remote_sem=sem["arr%d" % d], src=T.kv[:], dst=T["land%d" % d][:]))
-            total += cnt
+    pieces = _pieces(T, topo, r)
+    total = 0
+    if pieces:
         g.wait_ge(sem.kvl, 32)
-        g.remote_dma_fused(trs, local_sem=sem.sent)
+    for d, dst, lo, hi, mask, cnt, name, _ in pieces:
+        assert topo.may_write(core, dst)
+        rid, pid, _s = topo.addr(dst)
+        g.remote_dma(T["land%d" % d][:, lo:hi], T.kv[:, lo:hi], sem[name], sem.sent, pid, rid, mask)
+        total += cnt
 
-    srcs = sorted([d for d in range(1, WB + 1) if r - d >= 0], key=lambda d: (_far(topo, T.cores[r - d], core), d))
-    blocks = [(T.kv, None, 0)] + [(T["land%d" % d], sem["arr%d" % d], _plan(T, topo, r - d)[d][2]) for d in srcs]
+    remote = []
+    for d in range(1, WB + 1):
+        if r - d >= 0:
+            ps = [p for p in _pieces(T, topo, r - d) if p[0] == d]
+            remote.append(((ps[0][7], _far(topo, T.cores[r - d], core)), d, ps))
+    remote.sort()
+    blocks = [(T.kv, [], [])]
+    for _, d, ps in remote:
+        blocks.append((T["land%d" % d], [(sem[ps[0][6]], ps[0][5])], [(sem[p[6]], p[5]) for p in ps[1:]]))
     nb = len(blocks)
 
     def s_product(i):
-        buf, arr, cnt = blocks[i]
-        if arr is not None:
-            te.wait_ge(arr, cnt)
-        te.matmul(T["ps%d" % i][:, 0:D], buf[:, 0:D], T.qs[:], True, True).then_inc(sem["sm%d" % i], 1)
+        buf, kw, _ = blocks[i]
+        for s, n in kw:
+            te.wait_ge(s, n)
+        for h in range(2):
+            te.matmul(T["ps%d%d" % (i, h)][:, 0:H], buf[:, 0:D], T.qs[:, h * H:(h + 1) * H],
+                      True, True).then_inc(sem["sm%d%d" % (i, h)], 1)
 
     def o_product(i):
-        te.wait_ge(sem["rl%d" % i], 1)
-        te.matmul(T.po[:, 0:D], blocks[i][0][:, D:2 * D], T["s%d" % i][:], i == 0, i == nb - 1).then_inc(sem.om, 1)
+        buf, _, vw = blocks[i]
+        for s, n in vw:
+            te.wait_ge(s, n)
+        for h in range(2):
+            te.wait_ge(sem["rl%d%d" % (i, h)], 1)
+            te.matmul(T["po%d" % h][:, 0:H], buf[:, D:2 * D], T["s%d" % i][:, h * H:(h + 1) * H],
+                      i == 0, i == nb - 1).then_inc(sem["om%d" % h], 1)
 
     te.wait_ge(sem.kvl, 32)
     te.wait_ge(sem.ql, 16)
@@ -102,13 +117,16 @@ def rank_program(g, core, T, topo):
 
     ve.wait_ge(sem.zf, 1)
     for i in range(nb):
-        ve.wait_ge(sem["sm%d" % i], 1)
-        ve.tensor_tensor(T["s%d" % i][:], T["ps%d" % i][:, 0:D], T.zero[:], AluOpType.max).then_inc(sem["rl%d" % i], 1)
-    ve.wait_ge(sem.om, nb)
-    ve.tensor_copy(T.ys[:], T.po[:, 0:D]).then_inc(sem.cp, 1)
+        for h in range(2):
+            ve.wait_ge(sem["sm%d%d" % (i, h)], 1)
+            ve.tensor_tensor(T["s%d" % i][:, h * H:(h + 1) * H], T["ps%d%d" % (i, h)][:, 0:H], T.zero[:],
+                             AluOpType.max).then_inc(sem["rl%d%d" % (i, h)], 1)
+    for h in range(2):
+        ve.wait_ge(sem["om%d" % h], nb)
+        ve.tensor_copy(T.ys[:, h * H:(h + 1) * H], T["po%d" % h][:, 0:H]).then_inc(sem.cp, 1)
 
-    g.sync.wait_ge(sem.cp, 1)
+    g.sync.wait_ge(sem.cp, 2)
     g.sync.dma_start(T.y[:], T.ys[:]).then_inc(sem.stored, 16)
     g.sync.wait_ge(sem.stored, 16)
-    if plan:
+    if pieces:
         g.wait_ge(sem.sent, total)

from concourse.mybir import AluOpType

WB = 2
D = 128
H = D // 2
PER = 8

SCRATCH = {
    "kv": ("sbuf", [128, 2 * D], "bfloat16"),
    "qs": ("sbuf", [128, D], "bfloat16"),
    "land1": ("sbuf", [128, 2 * D], "bfloat16"),
    "land2": ("sbuf", [128, 2 * D], "bfloat16"),
    "zero": ("sbuf", [128, H], "float32"),
    "s0": ("sbuf", [128, D], "bfloat16"),
    "s1": ("sbuf", [128, D], "bfloat16"),
    "s2": ("sbuf", [128, D], "bfloat16"),
    "ys": ("sbuf", [128, D], "bfloat16"),
}
SEMAPHORES = ["kvl", "ql", "zf", "sent", "ka1", "ka2", "va1", "va2", "cp", "stored"]
for _h in range(2):
    SCRATCH["po%d" % _h] = ("psum", [128, 512], "float32")
    SEMAPHORES.append("om%d" % _h)
    for _i in range(WB + 1):
        SCRATCH["ps%d%d" % (_i, _h)] = ("psum", [128, 512], "float32")
        SEMAPHORES += ["sm%d%d" % (_i, _h), "rl%d%d" % (_i, _h)]


def _engines(mask):
    return [e for e in range(mask.bit_length()) if (mask >> e) & 1]


def _pieces(T, topo, r):
    src = T.cores[r]
    dsts = [(d, T.cores[r + d]) for d in range(1, WB + 1) if r + d < len(T.cores)]
    dsts.sort(key=lambda x: (len(_engines(topo.mask(src, x[1]))), x[0]))
    used, lane, line, out = [], [], 0, []
    for d, c in dsts:
        free = [e for e in _engines(topo.mask(src, c)) if e not in used]
        if len(free) >= PER:
            lane, line = free[:PER], 0
            used += lane
            cuts = [(0, 2 * D, "ka")]
        else:
            cuts = [(0, D, "ka"), (D, 2 * D, "va")]
        mask = sum(1 << e for e in lane)
        assert mask & topo.mask(src, c) == mask
        for lo, hi, name in cuts:
            line += hi - lo
            out.append((d, c, lo, hi, mask, len(lane), "%s%d" % (name, d), line))
    return out


def _far(topo, src, dst):
    if topo.chip(src) == topo.chip(dst):
        return 0
    return 1 if topo.die(src) == topo.die(dst) else 2


def rank_program(g, core, T, topo):
    r = T.rank_of(core)
    if r is None:
        return
    sem = T.sem
    te, ve = g.tensor, g.vector

    g.sync.dma_start(T.kv[:, 0:D], T.k[:]).then_inc(sem.kvl, 16)
    g.scalar.dma_start(T.kv[:, D:2 * D], T.v[:]).then_inc(sem.kvl, 16)
    g.sync.dma_start(T.qs[:], T.q[:]).then_inc(sem.ql, 16)
    ve.memset(T.zero[:], 0.0).then_inc(sem.zf, 1)

    pieces = _pieces(T, topo, r)
    total = 0
    if pieces:
        g.wait_ge(sem.kvl, 32)
    for d, dst, lo, hi, mask, cnt, name, _ in pieces:
        assert topo.may_write(core, dst)
        rid, pid, _s = topo.addr(dst)
        g.remote_dma(T["land%d" % d][:, lo:hi], T.kv[:, lo:hi], sem[name], sem.sent, pid, rid, mask)
        total += cnt

    remote = []
    for d in range(1, WB + 1):
        if r - d >= 0:
            ps = [p for p in _pieces(T, topo, r - d) if p[0] == d]
            remote.append(((ps[0][7], _far(topo, T.cores[r - d], core)), d, ps))
    remote.sort()
    blocks = [(T.kv, [], [])]
    for _, d, ps in remote:
        blocks.append((T["land%d" % d], [(sem[ps[0][6]], ps[0][5])], [(sem[p[6]], p[5]) for p in ps[1:]]))
    nb = len(blocks)

    def s_product(i):
        buf, kw, _ = blocks[i]
        for s, n in kw:
            te.wait_ge(s, n)
        for h in range(2):
            te.matmul(T["ps%d%d" % (i, h)][:, 0:H], buf[:, 0:D], T.qs[:, h * H:(h + 1) * H],
                      True, True).then_inc(sem["sm%d%d" % (i, h)], 1)

    def o_product(i):
        buf, _, vw = blocks[i]
        for s, n in vw:
            te.wait_ge(s, n)
        for h in range(2):
            te.wait_ge(sem["rl%d%d" % (i, h)], 1)
            te.matmul(T["po%d" % h][:, 0:H], buf[:, D:2 * D], T["s%d" % i][:, h * H:(h + 1) * H],
                      i == 0, i == nb - 1).then_inc(sem["om%d" % h], 1)

    te.wait_ge(sem.kvl, 32)
    te.wait_ge(sem.ql, 16)
    s_product(0)
    o_product(0)
    for i in range(1, nb):
        s_product(i)
    for i in range(1, nb):
        o_product(i)

    ve.wait_ge(sem.zf, 1)
    for i in range(nb):
        for h in range(2):
            ve.wait_ge(sem["sm%d%d" % (i, h)], 1)
            ve.tensor_tensor(T["s%d" % i][:, h * H:(h + 1) * H], T["ps%d%d" % (i, h)][:, 0:H], T.zero[:],
                             AluOpType.max).then_inc(sem["rl%d%d" % (i, h)], 1)
    for h in range(2):
        ve.wait_ge(sem["om%d" % h], nb)
        ve.tensor_copy(T.ys[:, h * H:(h + 1) * H], T["po%d" % h][:, 0:H]).then_inc(sem.cp, 1)

    g.sync.wait_ge(sem.cp, 2)
    g.sync.dma_start(T.y[:], T.ys[:]).then_inc(sem.stored, 16)
    g.sync.wait_ge(sem.stored, 16)
    if pieces:
        g.wait_ge(sem.sent, total)
